import numpy as np
import ml_dtypes


def mxq(x, axis, fmt="e4m3"):
    dtype, down = {"e4m3": (ml_dtypes.float8_e4m3fn, 7), "e5m2": (ml_dtypes.float8_e5m2, 14)}[fmt]
    v = np.moveaxis(np.asarray(x, np.float32).astype(ml_dtypes.bfloat16).astype(np.float64), axis, -1)
    blocks = v.reshape(v.shape[:-1] + (-1, 32))
    amax = np.abs(blocks).max(-1, keepdims=True)
    byte = np.maximum(np.where(amax > 0, np.frexp(amax)[1] - 1 + 127, 0) - down, 1)
    scale = np.exp2(byte - 127.0)
    codes = (blocks / scale).astype(np.float32).astype(dtype).astype(np.float64)
    return np.moveaxis((codes * scale).reshape(v.shape), -1, axis)


WIDE = False


def mx_kscale(k):
    if not WIDE:
        return np.ones(k)
    levels = np.array([10, -10, 5, -5, 0])
    if k % 512:
        return np.exp2(np.random.permutation(np.resize(levels, k // 32))).repeat(32)
    a = np.empty((k // 512, 16))
    for p in range(k // 512):
        a[p, :8] = np.random.permutation(np.resize(levels, 8))
        for g in range(8):
            far = levels[np.abs(levels - a[p, g]) >= 10]
            a[p, g + 8] = far[np.random.randint(len(far))]
    return np.exp2(a.ravel()).repeat(32)


def f64(x):
    return np.asarray(x).astype(np.float64)


def striped(idx):
    return np.tile(idx.reshape(-1, 16).T, (8, 1)).astype(np.uint16)


def unstriped(offs):
    return offs[:16].T.reshape(-1).astype(np.int64)


def pack_weight(w):
    k, n = w.shape
    w = f64(np.asarray(w, np.float32).astype(ml_dtypes.bfloat16)).reshape(k // 32, 32, n)
    amax = np.abs(w).max(1)
    byte = np.clip(np.where(amax > 0, np.frexp(amax)[1] - 1 + 127 - 7, 1), 1, 254)
    scaled = (w * np.exp2(127.0 - byte)[:, None, :]).reshape(k, n).astype(np.float32)
    words = np.ascontiguousarray(scaled.reshape(k // 512, 128, 4, n).transpose(0, 1, 3, 2)).astype(ml_dtypes.float8_e4m3fn).view(np.uint8)
    return words, np.ascontiguousarray(byte.astype(np.uint8).reshape(k // 512, 16, n))


def unpack_weight(words, scales):
    g, p, n, _ = words.shape
    vals = np.ascontiguousarray(words).view(ml_dtypes.float8_e4m3fn).astype(np.float64) * np.repeat(np.exp2(scales.astype(np.float64) - 127.0), 8, axis=1)[..., None]
    return vals.transpose(0, 1, 3, 2).reshape(g * 512, n)


def gelu(v):
    return 0.5 * v * (1.0 + np.tanh(np.sqrt(2.0 / np.pi) * (v + 0.044715 * v**3)))


K, T, N = 1024, 256, 256


def setup_inputs():
    n = np.random.standard_normal
    s = mx_kscale(K)[:, None]
    idx = np.random.permutation(K)
    x = n((T, K))
    x[:, idx] *= s[:, 0]
    words, scales = pack_weight(n((K, N)) / np.sqrt(K) / s)
    return {
        "x": x.astype(np.float32),
        "w_words": words,
        "w_scales": scales,
        "b": (0.3 * n((N, 1))).astype(np.float32),
        "offs": striped(idx),
    }


def reference(x, w_words, w_scales, b, offs):
    w = unpack_weight(w_words, w_scales)
    idx = unstriped(offs)
    xq = mxq(f64(x)[:, idx], 1, "e4m3").T
    return gelu((w.T @ xq) + f64(b))

import concourse.mybir as mybir
from concourse.masks import make_identity

K, T, N = 1024, 256, 256
P = 128
FLOPS = 2 * K * T * N

F32 = mybir.dt.float32
BF16 = mybir.dt.bfloat16
I32 = mybir.dt.int32
U16 = mybir.dt.uint16
U8 = mybir.dt.uint8
U32 = mybir.dt.uint32
FP8X4 = mybir.dt.float8_e4m3fn_x4
COPY = mybir.ActivationFunctionType.Copy
GELU = mybir.ActivationFunctionType.Gelu_apprx_tanh

K_PASS = 512
S_SHARE = 128
B_CHUNKS = ((0, 512), (512, 768), (768, 1024))


def tile_picked_actorder_lin_gelu_perm_l_kernel(tc, x, w_words, w_scales, b, offs, out):
    nc = tc.nc
    with (
        tc.tile_pool(name="lists", bufs=1) as lists,
        tc.tile_pool(name="keep", bufs=1) as keep,
        tc.psum_pool(name="psum", bufs=1) as psum,
    ):
        offsets = lists.tile([P, K // 16], U16, name="offsets")
        nc.sync.dma_start(offsets[:], offs)

        xa = keep.tile([P, K], F32, name="xa", align_bytes=64)
        xb = keep.tile([P, K], F32, name="xb", align_bytes=64)
        xb16 = keep.tile([P, K], BF16, name="xb16", align_bytes=64)
        nc.sync.dma_start(xa[:], x[0:P, :])
        for lo, hi in B_CHUNKS:
            nc.sync.dma_start(xb[:, lo:hi], x[P : 2 * P, lo:hi])

        words = keep.tile([P, 2, N], I32, name="words", align_bytes=64)
        nc.sync.dma_start(words[:], w_words.rearrange("a p m r -> p a (m r)").bitcast(I32))

        plane = keep.tile([P, N], U8, name="plane", align_bytes=64)
        nc.vector.memset(plane[:].bitcast(I32), 0)
        for q in range(4):
            nc.sync.dma_start(plane[32 * q : 32 * q + 8, :].bitcast(I32), w_scales[:, 4 * q : 4 * q + 4, :].bitcast(I32))
        bias = keep.tile([P, 2], F32, name="bias")
        with nc.allow_non_contiguous_dma("256 bias values, one a partition and output tile"):
            nc.sync.dma_start(bias[:], b.rearrange("(i p) o -> p (i o)", p=P))

        warm = keep.tile([P, 2], F32, name="warm")
        nc.vector.memset(warm[:, 0:1], 0.0)
        nc.scalar.activation(warm[:, 1:2], warm[:, 0:1], GELU)
        ident = keep.tile([P, P], F32, name="ident")
        make_identity(nc, ident[:])

        picked = [[keep.tile([P, K_PASS], BF16, name=f"picked{blk}{a}", align_bytes=64) for a in range(2)] for blk in range(2)]
        grouped = [[keep.tile([P, K_PASS], BF16, name=f"grouped{blk}{a}", align_bytes=64) for a in range(2)] for blk in range(2)]
        codes = [[keep.tile([P, P], U32, name=f"codes{blk}{a}", align_bytes=64) for a in range(2)] for blk in range(2)]
        scales = [[keep.tile([P, P], U8, name=f"scales{blk}{a}", align_bytes=64) for a in range(2)] for blk in range(2)]
        turned = [[psum.tile([P, 2, P], F32, name=f"turned{blk}{a}") for a in range(2)] for blk in range(2)]
        acc = [[psum.tile([P, P], F32, name=f"acc{blk}{i}") for i in range(2)] for blk in range(2)]
        result = [keep.tile([P, 2, P], F32, name=f"result{blk}") for blk in range(2)]

        def gather(engine, blk, a, lo, hi):
            source = (xa if blk == 0 else xb) if engine == "vector" else xb16
            looked_up = source[:].indirect(offsets[:, (K_PASS * a + lo) // 16 : (K_PASS * a + hi) // 16])
            dest = picked[blk][a][:].rearrange("q (u p v) -> q p u v", u=2, v=2)[:, lo // 4 : hi // 4]
            if engine == "vector":
                nc.vector.tensor_copy(dest, looked_up)
            else:
                nc.scalar.activation(dest, looked_up, COPY)

        def turn(blk, a):
            pairs = picked[blk][a][:].bitcast(F32)
            for u in range(2):
                nc.tensor.transpose(turned[blk][a][:, u, :], pairs[:, P * u : P * (u + 1)], ident[:])

        def interleave(engine, blk, a):
            dest = grouped[blk][a][:].bitcast(F32).rearrange("p (q u) -> p q u", u=2)
            source = turned[blk][a][:].rearrange("p u q -> p q u")
            if engine == "vector":
                nc.vector.tensor_copy(dest, source)
            else:
                nc.scalar.copy(dest, source)

        def quantize(blk, a):
            nc.vector.quantize_mx(out=codes[blk][a][:].bitcast(FP8X4), scales=scales[blk][a][:], in_=grouped[blk][a][:])

        def multiply(blk, a):
            for i in range(2):
                cols = slice(P * i, P * (i + 1))
                nc.tensor.matmul_mx(
                    out=acc[blk][i][:],
                    lhsT=words[:, a, cols].bitcast(FP8X4),
                    lhsT_scale=plane[4 * a : P, cols],
                    rhs=codes[blk][a][:].bitcast(FP8X4),
                    rhs_scale=scales[blk][a][:],
                    start=(a == 0),
                    stop=(a == 1),
                )

        def finish(blk, i):
            nc.scalar.activation(result[blk][:, i, :], acc[blk][i][:], GELU, bias=bias[:, i : i + 1])

        out_view = out.rearrange("(i p) t -> p i t", p=P)

        gather("vector", 0, 0, 0, 512)
        for lo, hi in B_CHUNKS:
            nc.scalar.copy(xb16[:, lo:hi], xb[:, lo:hi])
        turn(0, 0)
        gather("vector", 0, 1, 0, 512)
        interleave("scalar", 0, 0)
        gather("scalar", 1, 0, 0, 512)
        turn(0, 1)
        quantize(0, 0)
        multiply(0, 0)
        gather("vector", 1, 1, S_SHARE, 512)
        gather("scalar", 1, 1, 0, S_SHARE)
        turn(1, 0)
        interleave("scalar", 0, 1)
        quantize(0, 1)
        multiply(0, 1)
        interleave("scalar", 1, 0)
        turn(1, 1)
        quantize(1, 0)
        multiply(1, 0)
        interleave("scalar", 1, 1)
        quantize(1, 1)
        multiply(1, 1)
        for i in range(2):
            finish(0, i)
        nc.sync.dma_start(out_view[:, :, 0:P], result[0][:])
        for i in range(2):
            finish(1, i)
            nc.sync.dma_start(out_view[:, i, P : 2 * P], result[1][:, i, :])
